import numpy as np
import ml_dtypes


def mxq(x, axis, fmt="e4m3"):
    dtype, down = {"e4m3": (ml_dtypes.float8_e4m3fn, 7), "e5m2": (ml_dtypes.float8_e5m2, 14)}[fmt]
    v = np.moveaxis(np.asarray(x, np.float32).astype(ml_dtypes.bfloat16).astype(np.float64), axis, -1)
    blocks = v.reshape(v.shape[:-1] + (-1, 32))
    amax = np.abs(blocks).max(-1, keepdims=True)
    byte = np.maximum(np.where(amax > 0, np.frexp(amax)[1] - 1 + 127, 0) - down, 1)
    scale = np.exp2(byte - 127.0)
    codes = (blocks / scale).astype(np.float32).astype(dtype).astype(np.float64)
    return np.moveaxis((codes * scale).reshape(v.shape), -1, axis)


WIDE = False


def mx_kscale(k):
    if not WIDE:
        return np.ones(k)
    levels = np.array([30, -30])
    if k % 512:
        return np.exp2(np.random.permutation(np.resize(levels, k // 32))).repeat(32)
    a = np.empty((k // 512, 16))
    for p in range(k // 512):
        a[p, :8] = np.random.permutation(np.resize(levels, 8))
        for g in range(8):
            far = levels[np.abs(levels - a[p, g]) >= 10]
            a[p, g + 8] = far[np.random.randint(len(far))]
    return np.exp2(a.ravel()).repeat(32)


def f64(x):
    return np.asarray(x).astype(np.float64)


def striped(idx):
    return np.tile(np.asarray(idx).reshape(-1, 16).T, (8, 1)).astype(np.uint16)


def unstriped(offs):
    return offs[:16].T.reshape(-1).astype(np.int64)


E2M1 = np.array([0.0, 0.5, 1.0, 1.5, 2.0, 3.0, 4.0, 6.0, -0.0, -0.5, -1.0, -1.5, -2.0, -3.0, -4.0, -6.0])


def pack_weight(w, fmt):
    k, n = w.shape
    w = f64(np.asarray(w, np.float32).astype(ml_dtypes.bfloat16)).reshape(k // 32, 32, n)
    amax = np.abs(w).max(1)
    if fmt in ("e4m3", "e5m2"):
        byte = np.frexp(amax)[1] - 1 + 127 - (7 if fmt == "e4m3" else 14)
    else:
        mant, ex = np.frexp(amax / 6.0)
        byte = np.where(mant > 0.5, ex, ex - 1) + 127
    byte = np.clip(np.where(amax > 0, byte, 1), 1, 254)
    scaled = (w * np.exp2(127.0 - byte)[:, None, :]).reshape(k, n).astype(np.float32)
    by_word = np.ascontiguousarray(scaled.reshape(k // 512, 128, 4, n).transpose(0, 1, 3, 2))
    if fmt in ("e4m3", "e5m2"):
        words = by_word.astype(ml_dtypes.float8_e4m3fn if fmt == "e4m3" else ml_dtypes.float8_e5m2).view(np.uint8)
    else:
        c = by_word.astype(ml_dtypes.float4_e2m1fn).view(np.uint8) & 0xF
        words = (c[..., 0::2] | (c[..., 1::2] << 4)).reshape(k // 512, 128, 2 * n)
    return np.ascontiguousarray(words), np.ascontiguousarray(byte.astype(np.uint8).reshape(k // 512, 16, n))


def unpack_weight(words, scales, fmt):
    g, _, n = scales.shape
    words = np.ascontiguousarray(words).reshape(g, 128, n, -1)
    if fmt in ("e4m3", "e5m2"):
        vals = words.view(ml_dtypes.float8_e4m3fn if fmt == "e4m3" else ml_dtypes.float8_e5m2).astype(np.float64)
    else:
        nib = np.empty((g, 128, n, 4), np.uint8)
        nib[..., 0::2] = words & 0xF
        nib[..., 1::2] = words >> 4
        vals = E2M1[nib]
    vals = vals * np.repeat(np.exp2(scales.astype(np.float64) - 127.0), 8, axis=1)[..., None]
    return vals.transpose(0, 1, 3, 2).reshape(g * 512, n)


K, T, J, I, R, E, V = 512, 512, 256, 256, 512, 32, 512


def setup_inputs():
    n = np.random.standard_normal
    idx = np.random.permutation(T)[:J]
    idx2 = np.random.permutation(T)[:I]
    idx3 = np.random.permutation(V)[:I]
    fk = mx_kscale(K)
    fr = mx_kscale(R)
    xtp = pack_weight(n((K, T)) / fk[:, None], "e4m3")
    wap = pack_weight(n((K, R)) * 0.5 / np.sqrt(K) * fk[:, None] * fr, "e5m2")
    wbp = pack_weight(n((K, R)) * 1 / np.sqrt(K) * fk[:, None] / fr, "e2m1")
    return {
        "xt_words": xtp[0],
        "xt_scales": xtp[1],
        "wa_words": wap[0],
        "wa_scales": wap[1],
        "wb_words": wbp[0],
        "wb_scales": wbp[1],
        "tb": (n((R, V)) * 0.5 / fr[:, None]).astype(np.float32),
        "bi": (np.random.uniform(-15.0, 15.0, (1, I))).astype(np.float32),
        "offs": striped(idx),
        "offs2": striped(idx2),
        "offs3": striped(idx3),
    }


def reference(xt_words, xt_scales, wa_words, wa_scales, wb_words, wb_scales, tb, bi, offs, offs2, offs3):
    idx = unstriped(offs)
    idx2 = unstriped(offs2)
    idx3 = unstriped(offs3)
    xtu = unpack_weight(xt_words, xt_scales, "e4m3")
    wau = unpack_weight(wa_words, wa_scales, "e5m2")
    wbu = unpack_weight(wb_words, wb_scales, "e2m1")
    xtidxg = xtu[:, idx]
    za = wau.T @ xtidxg
    ma1 = za.reshape(R, E, J // E).mean(axis=2)
    ma2 = np.repeat(ma1, J // E, axis=1)
    ha = za - ma2
    xtidx2g = xtu[:, idx2]
    zb = wbu.T @ xtidx2g
    hb = np.maximum(zb - f64(tb)[:, idx3], 0.0)
    haq = mxq(ha, 0, "e4m3")
    hbq = mxq(hb, 0, "e5m2")
    a0 = haq.T @ hbq
    a = a0 + f64(bi)
    mn = np.mean(a, axis=1, keepdims=True)
    d = a - mn
    y = d / (np.mean(np.abs(d), axis=1, keepdims=True) + 4.0)
    return y

@@ -1,0 +1,248 @@
+from contextlib import ExitStack
+
+import concourse.mybir as mybir
+
+K, T, J, I, R, V = 512, 512, 256, 256, 512, 512
+FLOPS = 2 * K * R * (J + I) + 2 * R * J * I
+
+F32 = mybir.dt.float32
+BF16 = mybir.dt.bfloat16
+I32 = mybir.dt.int32
+U32 = mybir.dt.uint32
+U16 = mybir.dt.uint16
+U8 = mybir.dt.uint8
+E4M3 = mybir.dt.float8_e4m3fn_x4
+E5M2 = mybir.dt.float8_e5m2_x4
+E2M1 = mybir.dt.float4_e2m1fn_x4
+ALU = mybir.AluOpType
+ACT = mybir.ActivationFunctionType
+AX = mybir.AxisListType
+
+P = 128
+PACK = 4
+PAIR = 2
+BUNDLE = 8
+HALVES = 2
+
+
+def load_scales(queues, plane, scales):
+    for q in range(4):
+        queues[q].dma_start(
+            out=plane[32 * q : 32 * q + 4, :].bitcast(I32),
+            in_=scales[0, 4 * q : 4 * q + 4, :].bitcast(I32),
+        )
+
+
+def tile_list_meet_levelled_overtable_spread_kernel(
+    tc, xt_words, xt_scales, wa_words, wa_scales, wb_words, wb_scales, tb, bi, offs, offs2, offs3, out
+):
+    nc = tc.nc
+    with ExitStack() as ctx:
+        sb = ctx.enter_context(tc.tile_pool(name="sb", bufs=1))
+        ps = ctx.enter_context(tc.psum_pool(name="ps", bufs=1))
+
+        rows_list = sb.tile([P, J // 16], U16, name="rows_list")
+        cols_list = sb.tile([P, I // 16], U16, name="cols_list")
+        table_list = sb.tile([P, I // 16], U16, name="table_list")
+        x_words = sb.tile([P, T], U32, name="x_words", align_bytes=64)
+        x_scales = sb.tile([P, T], U8, name="x_scales", align_bytes=64)
+        wa_raw = sb.tile([P, R], U32, name="wa_raw", align_bytes=64)
+        wa_scales_raw = sb.tile([P, R], U8, name="wa_scales_raw", align_bytes=64)
+        wb_raw = sb.tile([P, R // PAIR], U32, name="wb_raw", tag="wb_then_bias", align_bytes=64)
+        wb_scales_raw = sb.tile([P, R], U8, name="wb_scales_raw", tag="scales_then_picked", align_bytes=64)
+        table = sb.tile([P, PACK * V], F32, name="table", align_bytes=64)
+        one = sb.tile([P, 1], F32, name="one")
+
+        nc.vector.memset(x_scales[:].bitcast(I32), 0)
+        nc.vector.memset(wa_scales_raw[:].bitcast(I32), 0)
+        nc.vector.memset(wb_scales_raw[:].bitcast(I32), 0)
+        nc.vector.memset(one[:], 1.0)
+
+        table_rows = tb.rearrange("(g t b) v -> b g t v", t=PACK, b=PAIR)
+        for b in range(PAIR):
+            nc.gpsimd.dma_start(
+                out=table[b:P:PAIR, :].rearrange("p (t v) -> p t v", t=PACK), in_=table_rows[b]
+            )
+
+        nc.sync.dma_start(rows_list[:], offs)
+        nc.scalar.dma_start(
+            out=x_words[:].bitcast(I32), in_=xt_words[0].rearrange("p n t -> p (n t)").bitcast(I32)
+        )
+        nc.scalar.dma_start(
+            out=wa_raw[:].bitcast(I32), in_=wa_words[0].rearrange("p n t -> p (n t)").bitcast(I32)
+        )
+        load_scales([nc.sync, nc.sync, nc.scalar, nc.scalar], x_scales, xt_scales)
+        nc.sync.dma_start(cols_list[:], offs2)
+        load_scales([nc.sync] * 4, wa_scales_raw, wa_scales)
+        nc.sync.dma_start(out=wb_raw[:].bitcast(I32), in_=wb_words[0].bitcast(I32))
+        nc.sync.dma_start(table_list[:], offs3)
+        load_scales([nc.sync] * 4, wb_scales_raw, wb_scales)
+
+        floor = sb.tile([P, 1], F32, name="floor")
+        nc.scalar.activation(out=floor[:], in_=one[:], func=ACT.Copy, scale=4.0 * I)
+
+        xa_words = sb.tile([P, J], U32, name="xa_words", align_bytes=64)
+        xa_scales = sb.tile([P, J], U8, name="xa_scales", align_bytes=64)
+        xb_words = sb.tile([P, I], U32, name="xb_words", align_bytes=64)
+        xb_scales = sb.tile([P, I], U8, name="xb_scales", align_bytes=64)
+        nc.vector.tensor_copy(xa_words[:], x_words[:].indirect(rows_list[:]))
+        nc.vector.tensor_copy(xa_scales[:], x_scales[:].indirect(rows_list[:]))
+        nc.vector.tensor_copy(xb_words[:], x_words[:].indirect(cols_list[:]))
+        nc.vector.tensor_copy(xb_scales[:], x_scales[:].indirect(cols_list[:]))
+
+        wa_dealt = sb.tile([P, R], U32, name="wa_dealt", align_bytes=64)
+        wa_scales_dealt = sb.tile([P, R], U8, name="wa_scales_dealt", align_bytes=64)
+        wb_dealt = sb.tile([P, 2 * R], U8, name="wb_dealt", align_bytes=64)
+        wb_scales_dealt = sb.tile([P, R], U8, name="wb_scales_dealt", align_bytes=64)
+        nc.scalar.copy(
+            out=wa_dealt[:].rearrange("p (t g b) -> p t g b", t=PACK, b=PAIR),
+            in_=wa_raw[:].rearrange("p (g t b) -> p t g b", t=PACK, b=PAIR),
+        )
+
+        def deal_pairs(dealt, raw):
+            nc.scalar.copy(
+                out=dealt.rearrange("p (t g) -> p t g", t=PACK),
+                in_=raw.rearrange("p (g t) -> p t g", t=PACK),
+            )
+
+        deal_pairs(wa_scales_dealt[:].bitcast(U16), wa_scales_raw[:].bitcast(U16))
+        deal_pairs(wb_dealt[:].bitcast(U32), wb_raw[:])
+        bias = sb.tile([P, I], F32, name="bias", tag="wb_then_bias", align_bytes=64)
+        nc.sync.dma_start(out=bias[:], in_=bi[0].partition_broadcast(P))
+
+        za = [ps.tile([P, PACK, P], F32, name=f"za{h}") for h in range(HALVES)]
+        zb = [ps.tile([P, 2, I], F32, name=f"zb{u}") for u in range(2)]
+        for h in range(HALVES):
+            cols = slice(P * h, P * (h + 1))
+            for t in range(PACK):
+                slot = slice(P * t, P * (t + 1))
+                nc.tensor.matmul_mx(
+                    out=za[h][:, t, :],
+                    lhsT=wa_dealt[:, slot].bitcast(E5M2),
+                    lhsT_scale=wa_scales_dealt[:, slot],
+                    rhs=xa_words[:, cols].bitcast(E4M3),
+                    rhs_scale=xa_scales[:, cols],
+                    start=True,
+                    stop=True,
+                )
+
+        def pick(picked, u):
+            for s in range(2):
+                t = 2 * u + s
+                nc.scalar.activation(
+                    out=picked[:, s, :],
+                    in_=table[:, V * t : V * (t + 1)].indirect(table_list[:]),
+                    func=ACT.Copy,
+                )
+
+        picked_low = sb.tile([P, 2, I], F32, name="picked_low", tag="picked_then_ha", align_bytes=64)
+        pick(picked_low, 0)
+        deal_pairs(wb_scales_dealt[:].bitcast(U16), wb_scales_raw[:].bitcast(U16))
+        picked_high = sb.tile([P, 2, I], F32, name="picked_high", tag="scales_then_picked", align_bytes=64)
+        pick(picked_high, 1)
+
+        for t in range(PACK):
+            nc.tensor.matmul_mx(
+                out=zb[t // 2][:, t % 2, :],
+                lhsT=wb_dealt[:, 2 * P * t : 2 * P * (t + 1)].bitcast(E2M1),
+                lhsT_scale=wb_scales_dealt[:, P * t : P * (t + 1)],
+                rhs=xb_words[:].bitcast(E4M3),
+                rhs_scale=xb_scales[:],
+                start=True,
+                stop=True,
+            )
+
+        bundles = P // BUNDLE
+        sums = [sb.tile([P, bundles, PACK], F32, name=f"sums{h}") for h in range(HALVES)]
+        means = [sb.tile([P, bundles, PACK], F32, name=f"means{h}") for h in range(HALVES)]
+        diff = sb.tile([P, PACK, I], F32, name="diff", align_bytes=64)
+        hb = [sb.tile([P, P * PACK], BF16, name=f"hb{h}", align_bytes=64) for h in range(HALVES)]
+        ha_words = sb.tile([P, J], U32, name="ha_words", align_bytes=64)
+        ha_scales = sb.tile([P, J], U8, name="ha_scales", align_bytes=64)
+        hb_words = sb.tile([P, I], U32, name="hb_words", align_bytes=64)
+        hb_scales = sb.tile([P, I], U8, name="hb_scales", align_bytes=64)
+
+        for h in range(HALVES):
+            nc.vector.tensor_reduce(
+                out=sums[h][:],
+                in_=za[h][:].rearrange("p t (e c) -> p e t c", c=BUNDLE),
+                axis=AX.X,
+                op=ALU.add,
+            )
+            nc.gpsimd.tensor_scalar(means[h][:], sums[h][:], 1.0 / BUNDLE, 0.0, ALU.mult, ALU.add)
+
+        def level(ha, h):
+            nc.vector.tensor_tensor(
+                out=ha[:].rearrange("p (e c t) -> p e c t", c=BUNDLE, t=PACK),
+                in0=za[h][:].rearrange("p t (e c) -> p e c t", c=BUNDLE),
+                in1=means[h][:].unsqueeze(2).to_broadcast([P, bundles, BUNDLE, PACK]),
+                op=ALU.subtract,
+            )
+
+        def quantize(words, scales, values, h, fmt):
+            cols = slice(P * h, P * (h + 1))
+            nc.vector.quantize_mx(out=words[:, cols].bitcast(fmt), scales=scales[:, cols], in_=values[:])
+
+        ha_first = sb.tile([P, P * PACK], BF16, name="ha_first", align_bytes=64)
+        level(ha_first, 0)
+        nc.vector.tensor_tensor(out=diff[:, 0:2, :], in0=zb[0][:], in1=picked_low[:], op=ALU.subtract)
+        for h in range(HALVES):
+            cols = slice(P * h, P * (h + 1))
+            nc.vector.tensor_tensor(
+                out=diff[:, 2:4, cols], in0=zb[1][:, :, cols], in1=picked_high[:, :, cols], op=ALU.subtract
+            )
+            nc.scalar.activation(
+                out=hb[h][:].rearrange("p (i t) -> p i t", t=PACK),
+                in_=diff[:, :, cols].rearrange("p t i -> p i t"),
+                func=ACT.Relu,
+            )
+        ha_second = sb.tile([P, P * PACK], BF16, name="ha_second", tag="picked_then_ha", align_bytes=64)
+        level(ha_second, 1)
+        quantize(ha_words, ha_scales, ha_first, 0, E4M3)
+        quantize(hb_words, hb_scales, hb[0], 0, E5M2)
+        quantize(ha_words, ha_scales, ha_second, 1, E4M3)
+        quantize(hb_words, hb_scales, hb[1], 1, E5M2)
+
+        a0 = [ps.tile([P, I], F32, name=f"a0{h}") for h in range(HALVES)]
+        a = [sb.tile([P, I], F32, name=f"a{h}", align_bytes=64) for h in range(HALVES)]
+        dev = [sb.tile([P, I], F32, name=f"dev{h}", align_bytes=64) for h in range(HALVES)]
+        size = [sb.tile([P, I], F32, name=f"size{h}", align_bytes=64) for h in range(HALVES)]
+        y = [sb.tile([P, I], F32, name=f"y{h}", align_bytes=64) for h in range(HALVES)]
+        total = [sb.tile([P, 1], F32, name=f"total{h}") for h in range(HALVES)]
+        spread = [sb.tile([P, 1], F32, name=f"spread{h}") for h in range(HALVES)]
+        divisor = [sb.tile([P, 1], F32, name=f"divisor{h}") for h in range(HALVES)]
+        inverse = [sb.tile([P, 1], F32, name=f"inverse{h}") for h in range(HALVES)]
+        for c in range(HALVES):
+            cols = slice(P * c, P * (c + 1))
+            for h in range(HALVES):
+                rows = slice(P * h, P * (h + 1))
+                nc.tensor.matmul_mx(
+                    out=a0[h][:, cols],
+                    lhsT=ha_words[:, rows].bitcast(E4M3),
+                    lhsT_scale=ha_scales[:, rows],
+                    rhs=hb_words[:, cols].bitcast(E5M2),
+                    rhs_scale=hb_scales[:, cols],
+                    start=True,
+                    stop=True,
+                )
+        for h in range(HALVES):
+            nc.vector.scalar_tensor_tensor(
+                a[h][:], a0[h][:], 1.0, bias[:], ALU.mult, ALU.add, accum_out=total[h][:]
+            )
+            nc.scalar.activation(
+                out=size[h][:],
+                in_=a[h][:],
+                func=ACT.Abs,
+                scale=-float(I),
+                bias=total[h][:],
+                accum_out=spread[h][:],
+            )
+        for h in range(HALVES):
+            nc.vector.tensor_scalar(dev[h][:], a[h][:], float(I), total[h][:], ALU.mult, ALU.subtract)
+        for h in range(HALVES):
+            nc.vector.tensor_scalar(divisor[h][:], spread[h][:], 1.0 / I, floor[:], ALU.mult, ALU.add)
+            nc.vector.reciprocal(inverse[h][:], divisor[h][:])
+        nc.vector.tensor_scalar(y[0][:], dev[0][:], inverse[0][:], None, ALU.mult)
+        nc.sync.dma_start(out=out[0:P, :], in_=y[0][:])
+        nc.scalar.activation(out=y[1][:], in_=dev[1][:], func=ACT.Copy, scale=inverse[1][:])
+        nc.sync.dma_start(out=out[P : 2 * P, :], in_=y[1][:])

@@ -25,9 +25,9 @@ BUNDLE = 8
 HALVES = 2
 
 
-def load_scales(queues, plane, scales):
-    for q in range(4):
-        queues[q].dma_start(
+def load_scales(queue, plane, scales, quadrants):
+    for q in quadrants:
+        queue.dma_start(
             out=plane[32 * q : 32 * q + 4, :].bitcast(I32),
             in_=scales[0, 4 * q : 4 * q + 4, :].bitcast(I32),
         )
@@ -48,35 +48,40 @@ def tile_list_meet_levelled_overtable_spread_kernel(
         x_scales = sb.tile([P, T], U8, name="x_scales", align_bytes=64)
         wa_raw = sb.tile([P, R], U32, name="wa_raw", align_bytes=64)
         wa_scales_raw = sb.tile([P, R], U8, name="wa_scales_raw", align_bytes=64)
-        wb_raw = sb.tile([P, R // PAIR], U32, name="wb_raw", tag="wb_then_bias", align_bytes=64)
-        wb_scales_raw = sb.tile([P, R], U8, name="wb_scales_raw", tag="scales_then_picked", align_bytes=64)
+        wb_raw = sb.tile([P, R // PAIR], U32, name="wb_raw", align_bytes=64)
+        wb_scales_raw = sb.tile([P, R], U8, name="wb_scales_raw", tag="scales_then_ha", align_bytes=64)
         table = sb.tile([P, PACK * V], F32, name="table", align_bytes=64)
         one = sb.tile([P, 1], F32, name="one")
 
-        nc.vector.memset(x_scales[:].bitcast(I32), 0)
+        nc.gpsimd.memset(x_scales[:].bitcast(I32), 0)
         nc.vector.memset(wa_scales_raw[:].bitcast(I32), 0)
         nc.vector.memset(wb_scales_raw[:].bitcast(I32), 0)
         nc.vector.memset(one[:], 1.0)
 
         table_rows = tb.rearrange("(g t b) v -> b g t v", t=PACK, b=PAIR)
-        for b in range(PAIR):
-            nc.gpsimd.dma_start(
-                out=table[b:P:PAIR, :].rearrange("p (t v) -> p t v", t=PACK), in_=table_rows[b]
-            )
 
-        nc.sync.dma_start(rows_list[:], offs)
-        nc.scalar.dma_start(
-            out=x_words[:].bitcast(I32), in_=xt_words[0].rearrange("p n t -> p (n t)").bitcast(I32)
-        )
-        nc.scalar.dma_start(
+        def load_table(queue, b):
+            queue.dma_start(out=table[b:P:PAIR, :].rearrange("p (t v) -> p t v", t=PACK), in_=table_rows[b])
+
+        nc.gpsimd.dma_start(
             out=wa_raw[:].bitcast(I32), in_=wa_words[0].rearrange("p n t -> p (n t)").bitcast(I32)
         )
-        load_scales([nc.sync, nc.sync, nc.scalar, nc.scalar], x_scales, xt_scales)
+        load_table(nc.gpsimd, 0)
+
+        nc.sync.dma_start(rows_list[:], offs)
+        load_scales(nc.sync, x_scales, xt_scales, (0, 1))
+        load_scales(nc.scalar, x_scales, xt_scales, (2, 3))
+        nc.sync.dma_start(
+            out=x_words[:].bitcast(I32), in_=xt_words[0].rearrange("p n t -> p (n t)").bitcast(I32)
+        )
+        load_scales(nc.sync, wa_scales_raw, wa_scales, range(4))
         nc.sync.dma_start(cols_list[:], offs2)
-        load_scales([nc.sync] * 4, wa_scales_raw, wa_scales)
+        load_table(nc.sync, 1)
         nc.sync.dma_start(out=wb_raw[:].bitcast(I32), in_=wb_words[0].bitcast(I32))
         nc.sync.dma_start(table_list[:], offs3)
-        load_scales([nc.sync] * 4, wb_scales_raw, wb_scales)
+        load_scales(nc.sync, wb_scales_raw, wb_scales, range(4))
+        bias = sb.tile([P, I], F32, name="bias", align_bytes=64)
+        nc.sync.dma_start(out=bias[:], in_=bi[0].partition_broadcast(P))
 
         floor = sb.tile([P, 1], F32, name="floor")
         nc.scalar.activation(out=floor[:], in_=one[:], func=ACT.Copy, scale=4.0 * I)
@@ -85,30 +90,32 @@ def tile_list_meet_levelled_overtable_spread_kernel(
         xa_scales = sb.tile([P, J], U8, name="xa_scales", align_bytes=64)
         xb_words = sb.tile([P, I], U32, name="xb_words", align_bytes=64)
         xb_scales = sb.tile([P, I], U8, name="xb_scales", align_bytes=64)
-        nc.vector.tensor_copy(xa_words[:], x_words[:].indirect(rows_list[:]))
-        nc.vector.tensor_copy(xa_scales[:], x_scales[:].indirect(rows_list[:]))
-        nc.vector.tensor_copy(xb_words[:], x_words[:].indirect(cols_list[:]))
-        nc.vector.tensor_copy(xb_scales[:], x_scales[:].indirect(cols_list[:]))
-
         wa_dealt = sb.tile([P, R], U32, name="wa_dealt", align_bytes=64)
         wa_scales_dealt = sb.tile([P, R], U8, name="wa_scales_dealt", align_bytes=64)
         wb_dealt = sb.tile([P, 2 * R], U8, name="wb_dealt", align_bytes=64)
         wb_scales_dealt = sb.tile([P, R], U8, name="wb_scales_dealt", align_bytes=64)
-        nc.scalar.copy(
-            out=wa_dealt[:].rearrange("p (t g b) -> p t g b", t=PACK, b=PAIR),
-            in_=wa_raw[:].rearrange("p (g t b) -> p t g b", t=PACK, b=PAIR),
-        )
 
-        def deal_pairs(dealt, raw):
-            nc.scalar.copy(
-                out=dealt.rearrange("p (t g) -> p t g", t=PACK),
-                in_=raw.rearrange("p (g t) -> p t g", t=PACK),
+        def deal_scales(dealt, raw):
+            nc.vector.tensor_copy(
+                out=dealt[:].bitcast(U16).rearrange("p (t g) -> p t g", t=PACK),
+                in_=raw[:].bitcast(U16).rearrange("p (g t) -> p t g", t=PACK),
             )
 
-        deal_pairs(wa_scales_dealt[:].bitcast(U16), wa_scales_raw[:].bitcast(U16))
-        deal_pairs(wb_dealt[:].bitcast(U32), wb_raw[:])
-        bias = sb.tile([P, I], F32, name="bias", tag="wb_then_bias", align_bytes=64)
-        nc.sync.dma_start(out=bias[:], in_=bi[0].partition_broadcast(P))
+        nc.vector.tensor_copy(xa_words[:], x_words[:].indirect(rows_list[:]))
+        nc.vector.tensor_copy(xa_scales[:], x_scales[:].indirect(rows_list[:]))
+        deal_scales(wa_scales_dealt, wa_scales_raw)
+        nc.vector.tensor_copy(xb_words[:], x_words[:].indirect(cols_list[:]))
+        nc.vector.tensor_copy(xb_scales[:], x_scales[:].indirect(cols_list[:]))
+
+        for u in range(2):
+            nc.scalar.copy(
+                out=wa_dealt[:].rearrange("p (t g b) -> p t g b", t=PACK, b=PAIR)[:, 2 * u : 2 * u + 2],
+                in_=wa_raw[:].rearrange("p (g t b) -> p t g b", t=PACK, b=PAIR)[:, 2 * u : 2 * u + 2],
+            )
+        nc.scalar.copy(
+            out=wb_dealt[:].bitcast(U32).rearrange("p (t g) -> p t g", t=PACK),
+            in_=wb_raw[:].rearrange("p (g t) -> p t g", t=PACK),
+        )
 
         za = [ps.tile([P, PACK, P], F32, name=f"za{h}") for h in range(HALVES)]
         zb = [ps.tile([P, 2, I], F32, name=f"zb{u}") for u in range(2)]
@@ -135,27 +142,16 @@ def tile_list_meet_levelled_overtable_spread_kernel(
                     func=ACT.Copy,
                 )
 
-        picked_low = sb.tile([P, 2, I], F32, name="picked_low", tag="picked_then_ha", align_bytes=64)
+        picked_low = sb.tile([P, 2, I], F32, name="picked_low", align_bytes=64)
         pick(picked_low, 0)
-        deal_pairs(wb_scales_dealt[:].bitcast(U16), wb_scales_raw[:].bitcast(U16))
-        picked_high = sb.tile([P, 2, I], F32, name="picked_high", tag="scales_then_picked", align_bytes=64)
+        picked_high = sb.tile([P, 2, I], F32, name="picked_high", align_bytes=64)
         pick(picked_high, 1)
-
-        for t in range(PACK):
-            nc.tensor.matmul_mx(
-                out=zb[t // 2][:, t % 2, :],
-                lhsT=wb_dealt[:, 2 * P * t : 2 * P * (t + 1)].bitcast(E2M1),
-                lhsT_scale=wb_scales_dealt[:, P * t : P * (t + 1)],
-                rhs=xb_words[:].bitcast(E4M3),
-                rhs_scale=xb_scales[:],
-                start=True,
-                stop=True,
-            )
 
         bundles = P // BUNDLE
         sums = [sb.tile([P, bundles, PACK], F32, name=f"sums{h}") for h in range(HALVES)]
         means = [sb.tile([P, bundles, PACK], F32, name=f"means{h}") for h in range(HALVES)]
-        diff = sb.tile([P, PACK, I], F32, name="diff", align_bytes=64)
+        diff_tile = sb.tile([P, HALVES * PACK * P], F32, name="diff", align_bytes=64)
+        diff = diff_tile[:].rearrange("p (h t i) -> p h t i", h=HALVES, t=PACK)
         hb = [sb.tile([P, P * PACK], BF16, name=f"hb{h}", align_bytes=64) for h in range(HALVES)]
         ha_words = sb.tile([P, J], U32, name="ha_words", align_bytes=64)
         ha_scales = sb.tile([P, J], U8, name="ha_scales", align_bytes=64)
@@ -169,11 +165,24 @@ def tile_list_meet_levelled_overtable_spread_kernel(
                 axis=AX.X,
                 op=ALU.add,
             )
-            nc.gpsimd.tensor_scalar(means[h][:], sums[h][:], 1.0 / BUNDLE, 0.0, ALU.mult, ALU.add)
+
+        nc.vector.tensor_scalar(means[0][:], sums[0][:], 1.0 / BUNDLE, None, ALU.mult)
+        nc.vector.tensor_scalar(means[1][:], sums[1][:], 1.0 / BUNDLE, None, ALU.mult)
+        deal_scales(wb_scales_dealt, wb_scales_raw)
+        for t in range(PACK):
+            nc.tensor.matmul_mx(
+                out=zb[t // 2][:, t % 2, :],
+                lhsT=wb_dealt[:, 2 * P * t : 2 * P * (t + 1)].bitcast(E2M1),
+                lhsT_scale=wb_scales_dealt[:, P * t : P * (t + 1)],
+                rhs=xb_words[:].bitcast(E4M3),
+                rhs_scale=xb_scales[:],
+                start=True,
+                stop=True,
+            )
 
         def level(ha, h):
             nc.vector.tensor_tensor(
-                out=ha[:].rearrange("p (e c t) -> p e c t", c=BUNDLE, t=PACK),
+                out=ha.rearrange("p (e c t) -> p e c t", c=BUNDLE, t=PACK),
                 in0=za[h][:].rearrange("p t (e c) -> p e c t", c=BUNDLE),
                 in1=means[h][:].unsqueeze(2).to_broadcast([P, bundles, BUNDLE, PACK]),
                 op=ALU.subtract,
@@ -181,27 +190,37 @@ def tile_list_meet_levelled_overtable_spread_kernel(
 
         def quantize(words, scales, values, h, fmt):
             cols = slice(P * h, P * (h + 1))
-            nc.vector.quantize_mx(out=words[:, cols].bitcast(fmt), scales=scales[:, cols], in_=values[:])
+            nc.vector.quantize_mx(out=words[:, cols].bitcast(fmt), scales=scales[:, cols], in_=values)
 
-        ha_first = sb.tile([P, P * PACK], BF16, name="ha_first", align_bytes=64)
-        level(ha_first, 0)
-        nc.vector.tensor_tensor(out=diff[:, 0:2, :], in0=zb[0][:], in1=picked_low[:], op=ALU.subtract)
+        ha = sb.tile([P, J * PACK], BF16, name="ha", tag="scales_then_ha", align_bytes=64)
+        for h in range(HALVES):
+            level(ha[:, P * PACK * h : P * PACK * (h + 1)], h)
+        nc.vector.quantize_mx(out=ha_words[:].bitcast(E4M3), scales=ha_scales[:], in_=ha[:])
+        nc.vector.tensor_tensor(
+            out=diff[:, :, 0:2, :],
+            in0=zb[0][:].rearrange("p t (h i) -> p h t i", h=HALVES),
+            in1=picked_low[:].rearrange("p t (h i) -> p h t i", h=HALVES),
+            op=ALU.subtract,
+        )
         for h in range(HALVES):
             cols = slice(P * h, P * (h + 1))
             nc.vector.tensor_tensor(
-                out=diff[:, 2:4, cols], in0=zb[1][:, :, cols], in1=picked_high[:, :, cols], op=ALU.subtract
+                out=diff[:, h, 2:4, :], in0=zb[1][:, :, cols], in1=picked_high[:, :, cols], op=ALU.subtract
             )
-            nc.scalar.activation(
-                out=hb[h][:].rearrange("p (i t) -> p i t", t=PACK),
-                in_=diff[:, :, cols].rearrange("p t i -> p i t"),
-                func=ACT.Relu,
-            )
-        ha_second = sb.tile([P, P * PACK], BF16, name="ha_second", tag="picked_then_ha", align_bytes=64)
-        level(ha_second, 1)
-        quantize(ha_words, ha_scales, ha_first, 0, E4M3)
-        quantize(hb_words, hb_scales, hb[0], 0, E5M2)
-        quantize(ha_words, ha_scales, ha_second, 1, E4M3)
-        quantize(hb_words, hb_scales, hb[1], 1, E5M2)
+        nc.scalar.activation(
+            out=hb[0][:].rearrange("p (i t) -> p i t", t=PACK),
+            in_=diff[:, 0].rearrange("p t i -> p i t"),
+            func=ACT.Relu,
+        )
+        nc.vector.tensor_scalar(
+            hb[1][:].rearrange("p (i t) -> p i t", t=PACK),
+            diff[:, 1].rearrange("p t i -> p i t"),
+            0.0,
+            None,
+            ALU.max,
+        )
+        quantize(hb_words, hb_scales, hb[0][:], 0, E5M2)
+        quantize(hb_words, hb_scales, hb[1][:], 1, E5M2)
 
         a0 = [ps.tile([P, I], F32, name=f"a0{h}") for h in range(HALVES)]
         a = [sb.tile([P, I], F32, name=f"a{h}", align_bytes=64) for h in range(HALVES)]
@@ -242,7 +261,6 @@ def tile_list_meet_levelled_overtable_spread_kernel(
         for h in range(HALVES):
             nc.vector.tensor_scalar(divisor[h][:], spread[h][:], 1.0 / I, floor[:], ALU.mult, ALU.add)
             nc.vector.reciprocal(inverse[h][:], divisor[h][:])
-        nc.vector.tensor_scalar(y[0][:], dev[0][:], inverse[0][:], None, ALU.mult)
-        nc.sync.dma_start(out=out[0:P, :], in_=y[0][:])
-        nc.scalar.activation(out=y[1][:], in_=dev[1][:], func=ACT.Copy, scale=inverse[1][:])
-        nc.sync.dma_start(out=out[P : 2 * P, :], in_=y[1][:])
+        for h in range(HALVES):
+            nc.vector.tensor_scalar(y[h][:], dev[h][:], inverse[h][:], None, ALU.mult)
+            nc.sync.dma_start(out=out[P * h : P * (h + 1), :], in_=y[h][:])

@@ -48,25 +48,20 @@ def tile_list_meet_levelled_overtable_spread_kernel(
         x_scales = sb.tile([P, T], U8, name="x_scales", align_bytes=64)
         wa_raw = sb.tile([P, R], U32, name="wa_raw", align_bytes=64)
         wa_scales_raw = sb.tile([P, R], U8, name="wa_scales_raw", align_bytes=64)
-        wb_raw = sb.tile([P, R // PAIR], U32, name="wb_raw", align_bytes=64)
+        wb_raw = sb.tile([P, R // PAIR], U32, name="wb_raw", tag="wb_then_bias", align_bytes=64)
         wb_scales_raw = sb.tile([P, R], U8, name="wb_scales_raw", tag="scales_then_ha", align_bytes=64)
         table = sb.tile([P, PACK * V], F32, name="table", align_bytes=64)
         one = sb.tile([P, 1], F32, name="one")
 
         nc.gpsimd.memset(x_scales[:].bitcast(I32), 0)
-        nc.vector.memset(wa_scales_raw[:].bitcast(I32), 0)
+        nc.gpsimd.memset(wa_scales_raw[:].bitcast(I32), 0)
         nc.vector.memset(wb_scales_raw[:].bitcast(I32), 0)
         nc.vector.memset(one[:], 1.0)
 
         table_rows = tb.rearrange("(g t b) v -> b g t v", t=PACK, b=PAIR)
 
-        def load_table(queue, b):
-            queue.dma_start(out=table[b:P:PAIR, :].rearrange("p (t v) -> p t v", t=PACK), in_=table_rows[b])
-
-        nc.gpsimd.dma_start(
-            out=wa_raw[:].bitcast(I32), in_=wa_words[0].rearrange("p n t -> p (n t)").bitcast(I32)
-        )
-        load_table(nc.gpsimd, 0)
+        def load_table(b):
+            nc.sync.dma_start(out=table[b:P:PAIR, :].rearrange("p (t v) -> p t v", t=PACK), in_=table_rows[b])
 
         nc.sync.dma_start(rows_list[:], offs)
         load_scales(nc.sync, x_scales, xt_scales, (0, 1))
@@ -74,14 +69,16 @@ def tile_list_meet_levelled_overtable_spread_kernel(
         nc.sync.dma_start(
             out=x_words[:].bitcast(I32), in_=xt_words[0].rearrange("p n t -> p (n t)").bitcast(I32)
         )
-        load_scales(nc.sync, wa_scales_raw, wa_scales, range(4))
         nc.sync.dma_start(cols_list[:], offs2)
-        load_table(nc.sync, 1)
-        nc.sync.dma_start(out=wb_raw[:].bitcast(I32), in_=wb_words[0].bitcast(I32))
+        nc.sync.dma_start(
+            out=wa_raw[:].bitcast(I32), in_=wa_words[0].rearrange("p n t -> p (n t)").bitcast(I32)
+        )
+        load_scales(nc.sync, wa_scales_raw, wa_scales, range(4))
+        load_table(0)
         nc.sync.dma_start(table_list[:], offs3)
+        load_table(1)
+        nc.sync.dma_start(out=wb_raw[:].bitcast(I32), in_=wb_words[0].bitcast(I32))
         load_scales(nc.sync, wb_scales_raw, wb_scales, range(4))
-        bias = sb.tile([P, I], F32, name="bias", align_bytes=64)
-        nc.sync.dma_start(out=bias[:], in_=bi[0].partition_broadcast(P))
 
         floor = sb.tile([P, 1], F32, name="floor")
         nc.scalar.activation(out=floor[:], in_=one[:], func=ACT.Copy, scale=4.0 * I)
@@ -97,25 +94,25 @@ def tile_list_meet_levelled_overtable_spread_kernel(
 
         def deal_scales(dealt, raw):
             nc.vector.tensor_copy(
-                out=dealt[:].bitcast(U16).rearrange("p (t g) -> p t g", t=PACK),
-                in_=raw[:].bitcast(U16).rearrange("p (g t) -> p t g", t=PACK),
+                out=dealt[:].bitcast(U16).rearrange("p (t n g) -> p n t g", t=PACK, g=8),
+                in_=raw[:].bitcast(U16).rearrange("p (n g t) -> p n t g", t=PACK, g=8),
             )
 
         nc.vector.tensor_copy(xa_words[:], x_words[:].indirect(rows_list[:]))
         nc.vector.tensor_copy(xa_scales[:], x_scales[:].indirect(rows_list[:]))
-        deal_scales(wa_scales_dealt, wa_scales_raw)
         nc.vector.tensor_copy(xb_words[:], x_words[:].indirect(cols_list[:]))
         nc.vector.tensor_copy(xb_scales[:], x_scales[:].indirect(cols_list[:]))
 
         for u in range(2):
             nc.scalar.copy(
-                out=wa_dealt[:].rearrange("p (t g b) -> p t g b", t=PACK, b=PAIR)[:, 2 * u : 2 * u + 2],
-                in_=wa_raw[:].rearrange("p (g t b) -> p t g b", t=PACK, b=PAIR)[:, 2 * u : 2 * u + 2],
+                out=wa_dealt[:].rearrange("p (t n g b) -> p n t g b", t=PACK, g=4, b=PAIR)[:, :, 2 * u : 2 * u + 2],
+                in_=wa_raw[:].rearrange("p (n g t b) -> p n t g b", t=PACK, g=4, b=PAIR)[:, :, 2 * u : 2 * u + 2],
             )
-        nc.scalar.copy(
-            out=wb_dealt[:].bitcast(U32).rearrange("p (t g) -> p t g", t=PACK),
-            in_=wb_raw[:].rearrange("p (g t) -> p t g", t=PACK),
-        )
+        for u in range(2):
+            nc.scalar.copy(
+                out=wa_scales_dealt[:].bitcast(U16).rearrange("p (t n g) -> p n t g", t=PACK, g=8)[:, :, 2 * u : 2 * u + 2],
+                in_=wa_scales_raw[:].bitcast(U16).rearrange("p (n g t) -> p n t g", t=PACK, g=8)[:, :, 2 * u : 2 * u + 2],
+            )
 
         za = [ps.tile([P, PACK, P], F32, name=f"za{h}") for h in range(HALVES)]
         zb = [ps.tile([P, 2, I], F32, name=f"zb{u}") for u in range(2)]
@@ -165,10 +162,15 @@ def tile_list_meet_levelled_overtable_spread_kernel(
                 axis=AX.X,
                 op=ALU.add,
             )
+            nc.gpsimd.tensor_scalar(means[h][:], sums[h][:], 1.0 / BUNDLE, 0.0, ALU.mult, ALU.add)
 
-        nc.vector.tensor_scalar(means[0][:], sums[0][:], 1.0 / BUNDLE, None, ALU.mult)
-        nc.vector.tensor_scalar(means[1][:], sums[1][:], 1.0 / BUNDLE, None, ALU.mult)
+        nc.vector.tensor_copy(
+            out=wb_dealt[:].bitcast(I32).rearrange("p (t n g) -> p n t g", t=PACK, g=4),
+            in_=wb_raw[:].bitcast(I32).rearrange("p (n g t) -> p n t g", t=PACK, g=4),
+        )
         deal_scales(wb_scales_dealt, wb_scales_raw)
+        bias = sb.tile([P, I], F32, name="bias", tag="wb_then_bias", align_bytes=64)
+        nc.sync.dma_start(out=bias[:], in_=bi[0].partition_broadcast(P))
         for t in range(PACK):
             nc.tensor.matmul_mx(
                 out=zb[t // 2][:, t % 2, :],

@@ -20,7 +20,6 @@ AX = mybir.AxisListType
 
 P = 128
 PACK = 4
-PAIR = 2
 BUNDLE = 8
 HALVES = 2
 
@@ -39,6 +38,7 @@ def tile_list_meet_levelled_overtable_spread_kernel(
     nc = tc.nc
     with ExitStack() as ctx:
         sb = ctx.enter_context(tc.tile_pool(name="sb", bufs=1))
+        reused = ctx.enter_context(tc.tile_pool(name="reused", bufs=1))
         ps = ctx.enter_context(tc.psum_pool(name="ps", bufs=1))
 
         rows_list = sb.tile([P, J // 16], U16, name="rows_list")
@@ -48,9 +48,9 @@ def tile_list_meet_levelled_overtable_spread_kernel(
         x_scales = sb.tile([P, T], U8, name="x_scales", align_bytes=64)
         wa_raw = sb.tile([P, R], U32, name="wa_raw", align_bytes=64)
         wa_scales_raw = sb.tile([P, R], U8, name="wa_scales_raw", align_bytes=64)
-        wb_raw = sb.tile([P, R // PAIR], U32, name="wb_raw", tag="wb_then_bias", align_bytes=64)
-        wb_scales_raw = sb.tile([P, R], U8, name="wb_scales_raw", tag="scales_then_ha", align_bytes=64)
-        table = sb.tile([P, PACK * V], F32, name="table", align_bytes=64)
+        wb_raw = sb.tile([P, 2 * R], U8, name="wb_raw", align_bytes=64)
+        wb_scales_raw = reused.tile([P, R], U8, name="wb_scales_raw", offset=0, align_bytes=64)
+        table = [sb.tile([P, 2 * V], F32, name=f"table{u}", align_bytes=64) for u in range(2)]
         one = sb.tile([P, 1], F32, name="one")
 
         nc.gpsimd.memset(x_scales[:].bitcast(I32), 0)
@@ -58,10 +58,7 @@ def tile_list_meet_levelled_overtable_spread_kernel(
         nc.vector.memset(wb_scales_raw[:].bitcast(I32), 0)
         nc.vector.memset(one[:], 1.0)
 
-        table_rows = tb.rearrange("(g t b) v -> b g t v", t=PACK, b=PAIR)
-
-        def load_table(b):
-            nc.sync.dma_start(out=table[b:P:PAIR, :].rearrange("p (t v) -> p t v", t=PACK), in_=table_rows[b])
+        table_rows = tb.rearrange("(p u s) v -> u p (s v)", u=2, s=2)
 
         nc.sync.dma_start(rows_list[:], offs)
         load_scales(nc.sync, x_scales, xt_scales, (0, 1))
@@ -69,16 +66,17 @@ def tile_list_meet_levelled_overtable_spread_kernel(
         nc.sync.dma_start(
             out=x_words[:].bitcast(I32), in_=xt_words[0].rearrange("p n t -> p (n t)").bitcast(I32)
         )
-        nc.sync.dma_start(cols_list[:], offs2)
+        load_scales(nc.sync, wa_scales_raw, wa_scales, (0,))
         nc.sync.dma_start(
             out=wa_raw[:].bitcast(I32), in_=wa_words[0].rearrange("p n t -> p (n t)").bitcast(I32)
         )
-        load_scales(nc.sync, wa_scales_raw, wa_scales, range(4))
-        load_table(0)
-        nc.sync.dma_start(table_list[:], offs3)
-        load_table(1)
+        load_scales(nc.sync, wa_scales_raw, wa_scales, (1, 2, 3))
+        nc.sync.dma_start(cols_list[:], offs2)
         nc.sync.dma_start(out=wb_raw[:].bitcast(I32), in_=wb_words[0].bitcast(I32))
+        nc.sync.dma_start(out=table[0][:], in_=table_rows[0])
+        nc.sync.dma_start(table_list[:], offs3)
         load_scales(nc.sync, wb_scales_raw, wb_scales, range(4))
+        nc.sync.dma_start(out=table[1][:], in_=table_rows[1])
 
         floor = sb.tile([P, 1], F32, name="floor")
         nc.scalar.activation(out=floor[:], in_=one[:], func=ACT.Copy, scale=4.0 * I)
@@ -92,26 +90,23 @@ def tile_list_meet_levelled_overtable_spread_kernel(
         wb_dealt = sb.tile([P, 2 * R], U8, name="wb_dealt", align_bytes=64)
         wb_scales_dealt = sb.tile([P, R], U8, name="wb_scales_dealt", align_bytes=64)
 
-        def deal_scales(dealt, raw):
+        def deal_scales(dealt, raw, slots):
             nc.vector.tensor_copy(
-                out=dealt[:].bitcast(U16).rearrange("p (t n g) -> p n t g", t=PACK, g=8),
-                in_=raw[:].bitcast(U16).rearrange("p (n g t) -> p n t g", t=PACK, g=8),
+                out=dealt[:].rearrange("p (t n g) -> p n t g", t=PACK, g=16)[:, :, slots],
+                in_=raw[:].rearrange("p (n g t) -> p n t g", t=PACK, g=16)[:, :, slots],
             )
 
         nc.vector.tensor_copy(xa_words[:], x_words[:].indirect(rows_list[:]))
         nc.vector.tensor_copy(xa_scales[:], x_scales[:].indirect(rows_list[:]))
+        deal_scales(wa_scales_dealt, wa_scales_raw, slice(0, 2))
+        deal_scales(wa_scales_dealt, wa_scales_raw, slice(2, 4))
         nc.vector.tensor_copy(xb_words[:], x_words[:].indirect(cols_list[:]))
         nc.vector.tensor_copy(xb_scales[:], x_scales[:].indirect(cols_list[:]))
 
         for u in range(2):
             nc.scalar.copy(
-                out=wa_dealt[:].rearrange("p (t n g b) -> p n t g b", t=PACK, g=4, b=PAIR)[:, :, 2 * u : 2 * u + 2],
-                in_=wa_raw[:].rearrange("p (n g t b) -> p n t g b", t=PACK, g=4, b=PAIR)[:, :, 2 * u : 2 * u + 2],
-            )
-        for u in range(2):
-            nc.scalar.copy(
-                out=wa_scales_dealt[:].bitcast(U16).rearrange("p (t n g) -> p n t g", t=PACK, g=8)[:, :, 2 * u : 2 * u + 2],
-                in_=wa_scales_raw[:].bitcast(U16).rearrange("p (n g t) -> p n t g", t=PACK, g=8)[:, :, 2 * u : 2 * u + 2],
+                out=wa_dealt[:].rearrange("p (t n g) -> p n t g", t=PACK, g=4)[:, :, 2 * u : 2 * u + 2],
+                in_=wa_raw[:].rearrange("p (n g t) -> p n t g", t=PACK, g=4)[:, :, 2 * u : 2 * u + 2],
             )
 
         za = [ps.tile([P, PACK, P], F32, name=f"za{h}") for h in range(HALVES)]
@@ -132,30 +127,33 @@ def tile_list_meet_levelled_overtable_spread_kernel(
 
         def pick(picked, u):
             for s in range(2):
-                t = 2 * u + s
                 nc.scalar.activation(
                     out=picked[:, s, :],
-                    in_=table[:, V * t : V * (t + 1)].indirect(table_list[:]),
+                    in_=table[u][:, V * s : V * (s + 1)].indirect(table_list[:]),
                     func=ACT.Copy,
                 )
 
         picked_low = sb.tile([P, 2, I], F32, name="picked_low", align_bytes=64)
+        nc.scalar.copy(
+            out=wb_dealt[:].bitcast(U16).rearrange("p (t n g) -> p n t g", t=PACK, g=8),
+            in_=wb_raw[:].bitcast(U16).rearrange("p (n g t) -> p n t g", t=PACK, g=8),
+        )
         pick(picked_low, 0)
-        picked_high = sb.tile([P, 2, I], F32, name="picked_high", align_bytes=64)
-        pick(picked_high, 1)
 
         bundles = P // BUNDLE
-        sums = [sb.tile([P, bundles, PACK], F32, name=f"sums{h}") for h in range(HALVES)]
+        sums = [
+            sb.tile([P, bundles, PACK], F32, name="sums0", tag="sums0", align_bytes=64),
+            reused.tile([P, bundles, PACK], F32, name="sums1", offset=0, align_bytes=64),
+        ]
         means = [sb.tile([P, bundles, PACK], F32, name=f"means{h}") for h in range(HALVES)]
         diff_tile = sb.tile([P, HALVES * PACK * P], F32, name="diff", align_bytes=64)
         diff = diff_tile[:].rearrange("p (h t i) -> p h t i", h=HALVES, t=PACK)
         hb = [sb.tile([P, P * PACK], BF16, name=f"hb{h}", align_bytes=64) for h in range(HALVES)]
         ha_words = sb.tile([P, J], U32, name="ha_words", align_bytes=64)
-        ha_scales = sb.tile([P, J], U8, name="ha_scales", align_bytes=64)
         hb_words = sb.tile([P, I], U32, name="hb_words", align_bytes=64)
         hb_scales = sb.tile([P, I], U8, name="hb_scales", align_bytes=64)
 
-        for h in range(HALVES):
+        def bundle_means(h):
             nc.vector.tensor_reduce(
                 out=sums[h][:],
                 in_=za[h][:].rearrange("p t (e c) -> p e t c", c=BUNDLE),
@@ -164,12 +162,15 @@ def tile_list_meet_levelled_overtable_spread_kernel(
             )
             nc.gpsimd.tensor_scalar(means[h][:], sums[h][:], 1.0 / BUNDLE, 0.0, ALU.mult, ALU.add)
 
-        nc.vector.tensor_copy(
-            out=wb_dealt[:].bitcast(I32).rearrange("p (t n g) -> p n t g", t=PACK, g=4),
-            in_=wb_raw[:].bitcast(I32).rearrange("p (n g t) -> p n t g", t=PACK, g=4),
-        )
-        deal_scales(wb_scales_dealt, wb_scales_raw)
-        bias = sb.tile([P, I], F32, name="bias", tag="wb_then_bias", align_bytes=64)
+        bundle_means(0)
+        deal_scales(wb_scales_dealt, wb_scales_raw, slice(0, 4))
+        bundle_means(1)
+        ha_words32 = J * PACK // 2
+        shared = reused.tile([P, ha_words32 - P + 2 * I], F32, name="shared", offset=R // 2, align_bytes=64)
+        ha = shared[:, 0:ha_words32].bitcast(BF16)
+        picked_high = shared[:, ha_words32 - P :].rearrange("p (s i) -> p s i", s=2)
+        pick(picked_high, 1)
+        bias = sb.tile([P, I], F32, name="bias", tag="sums0", align_bytes=64)
         nc.sync.dma_start(out=bias[:], in_=bi[0].partition_broadcast(P))
         for t in range(PACK):
             nc.tensor.matmul_mx(
@@ -194,10 +195,8 @@ def tile_list_meet_levelled_overtable_spread_kernel(
             cols = slice(P * h, P * (h + 1))
             nc.vector.quantize_mx(out=words[:, cols].bitcast(fmt), scales=scales[:, cols], in_=values)
 
-        ha = sb.tile([P, J * PACK], BF16, name="ha", tag="scales_then_ha", align_bytes=64)
-        for h in range(HALVES):
-            level(ha[:, P * PACK * h : P * PACK * (h + 1)], h)
-        nc.vector.quantize_mx(out=ha_words[:].bitcast(E4M3), scales=ha_scales[:], in_=ha[:])
+        ha_scales = sb.tile([P, J], U8, name="ha_scales", align_bytes=64)
+        level(ha[:, 0 : P * PACK], 0)
         nc.vector.tensor_tensor(
             out=diff[:, :, 0:2, :],
             in0=zb[0][:].rearrange("p t (h i) -> p h t i", h=HALVES),
@@ -209,19 +208,14 @@ def tile_list_meet_levelled_overtable_spread_kernel(
             nc.vector.tensor_tensor(
                 out=diff[:, h, 2:4, :], in0=zb[1][:, :, cols], in1=picked_high[:, :, cols], op=ALU.subtract
             )
-        nc.scalar.activation(
-            out=hb[0][:].rearrange("p (i t) -> p i t", t=PACK),
-            in_=diff[:, 0].rearrange("p t i -> p i t"),
-            func=ACT.Relu,
-        )
-        nc.vector.tensor_scalar(
-            hb[1][:].rearrange("p (i t) -> p i t", t=PACK),
-            diff[:, 1].rearrange("p t i -> p i t"),
-            0.0,
-            None,
-            ALU.max,
-        )
+            nc.scalar.activation(
+                out=hb[h][:].rearrange("p (i t) -> p i t", t=PACK),
+                in_=diff[:, h].rearrange("p t i -> p i t"),
+                func=ACT.Relu,
+            )
+        level(ha[:, P * PACK :], 1)
         quantize(hb_words, hb_scales, hb[0][:], 0, E5M2)
+        nc.vector.quantize_mx(out=ha_words[:].bitcast(E4M3), scales=ha_scales[:], in_=ha)
         quantize(hb_words, hb_scales, hb[1][:], 1, E5M2)
 
         a0 = [ps.tile([P, I], F32, name=f"a0{h}") for h in range(HALVES)]

@@ -77,6 +77,8 @@ def tile_list_meet_levelled_overtable_spread_kernel(
         nc.sync.dma_start(table_list[:], offs3)
         load_scales(nc.sync, wb_scales_raw, wb_scales, range(4))
         nc.sync.dma_start(out=table[1][:], in_=table_rows[1])
+        bias = sb.tile([P, I], F32, name="bias", align_bytes=64)
+        nc.sync.dma_start(out=bias[:], in_=bi[0].partition_broadcast(P))
 
         floor = sb.tile([P, 1], F32, name="floor")
         nc.scalar.activation(out=floor[:], in_=one[:], func=ACT.Copy, scale=4.0 * I)
@@ -142,7 +144,7 @@ def tile_list_meet_levelled_overtable_spread_kernel(
 
         bundles = P // BUNDLE
         sums = [
-            sb.tile([P, bundles, PACK], F32, name="sums0", tag="sums0", align_bytes=64),
+            sb.tile([P, bundles, PACK], F32, name="sums0", align_bytes=64),
             reused.tile([P, bundles, PACK], F32, name="sums1", offset=0, align_bytes=64),
         ]
         means = [sb.tile([P, bundles, PACK], F32, name=f"means{h}") for h in range(HALVES)]
@@ -170,8 +172,6 @@ def tile_list_meet_levelled_overtable_spread_kernel(
         ha = shared[:, 0:ha_words32].bitcast(BF16)
         picked_high = shared[:, ha_words32 - P :].rearrange("p (s i) -> p s i", s=2)
         pick(picked_high, 1)
-        bias = sb.tile([P, I], F32, name="bias", tag="sums0", align_bytes=64)
-        nc.sync.dma_start(out=bias[:], in_=bi[0].partition_broadcast(P))
         for t in range(PACK):
             nc.tensor.matmul_mx(
                 out=zb[t // 2][:, t % 2, :],
@@ -209,8 +209,8 @@ def tile_list_meet_levelled_overtable_spread_kernel(
                 out=diff[:, h, 2:4, :], in0=zb[1][:, :, cols], in1=picked_high[:, :, cols], op=ALU.subtract
             )
             nc.scalar.activation(
-                out=hb[h][:].rearrange("p (i t) -> p i t", t=PACK),
-                in_=diff[:, h].rearrange("p t i -> p i t"),
+                out=hb[h][:].rearrange("p (n g t) -> p n t g", g=4, t=PACK),
+                in_=diff[:, h].rearrange("p t (n g) -> p n t g", g=4),
                 func=ACT.Relu,
             )
         level(ha[:, P * PACK :], 1)

from contextlib import ExitStack

import concourse.mybir as mybir

K, T, J, I, R, V = 512, 512, 256, 256, 512, 512
FLOPS = 2 * K * R * (J + I) + 2 * R * J * I

F32 = mybir.dt.float32
BF16 = mybir.dt.bfloat16
I32 = mybir.dt.int32
U32 = mybir.dt.uint32
U16 = mybir.dt.uint16
U8 = mybir.dt.uint8
E4M3 = mybir.dt.float8_e4m3fn_x4
E5M2 = mybir.dt.float8_e5m2_x4
E2M1 = mybir.dt.float4_e2m1fn_x4
ALU = mybir.AluOpType
ACT = mybir.ActivationFunctionType
AX = mybir.AxisListType

P = 128
PACK = 4
BUNDLE = 8
HALVES = 2


def load_scales(queue, plane, scales, quadrants):
    for q in quadrants:
        queue.dma_start(
            out=plane[32 * q : 32 * q + 4, :].bitcast(I32),
            in_=scales[0, 4 * q : 4 * q + 4, :].bitcast(I32),
        )


def tile_list_meet_levelled_overtable_spread_kernel(
    tc, xt_words, xt_scales, wa_words, wa_scales, wb_words, wb_scales, tb, bi, offs, offs2, offs3, out
):
    nc = tc.nc
    with ExitStack() as ctx:
        sb = ctx.enter_context(tc.tile_pool(name="sb", bufs=1))
        reused = ctx.enter_context(tc.tile_pool(name="reused", bufs=1))
        ps = ctx.enter_context(tc.psum_pool(name="ps", bufs=1))

        rows_list = sb.tile([P, J // 16], U16, name="rows_list")
        cols_list = sb.tile([P, I // 16], U16, name="cols_list")
        table_list = sb.tile([P, I // 16], U16, name="table_list")
        x_words = sb.tile([P, T], U32, name="x_words", align_bytes=64)
        x_scales = sb.tile([P, T], U8, name="x_scales", align_bytes=64)
        wa_raw = sb.tile([P, R], U32, name="wa_raw", align_bytes=64)
        wa_scales_raw = sb.tile([P, R], U8, name="wa_scales_raw", align_bytes=64)
        wb_raw = sb.tile([P, 2 * R], U8, name="wb_raw", align_bytes=64)
        wb_scales_raw = reused.tile([P, R], U8, name="wb_scales_raw", offset=0, align_bytes=64)
        table = [sb.tile([P, 2 * V], F32, name=f"table{u}", align_bytes=64) for u in range(2)]
        one = sb.tile([P, 1], F32, name="one")

        nc.gpsimd.memset(x_scales[:].bitcast(I32), 0)
        nc.gpsimd.memset(wa_scales_raw[:].bitcast(I32), 0)
        nc.vector.memset(wb_scales_raw[:].bitcast(I32), 0)
        nc.vector.memset(one[:], 1.0)

        table_rows = tb.rearrange("(p u s) v -> u p (s v)", u=2, s=2)

        nc.sync.dma_start(rows_list[:], offs)
        load_scales(nc.sync, x_scales, xt_scales, (0, 1))
        load_scales(nc.scalar, x_scales, xt_scales, (2, 3))
        nc.sync.dma_start(
            out=x_words[:].bitcast(I32), in_=xt_words[0].rearrange("p n t -> p (n t)").bitcast(I32)
        )
        load_scales(nc.sync, wa_scales_raw, wa_scales, (0,))
        nc.sync.dma_start(
            out=wa_raw[:].bitcast(I32), in_=wa_words[0].rearrange("p n t -> p (n t)").bitcast(I32)
        )
        load_scales(nc.sync, wa_scales_raw, wa_scales, (1, 2, 3))
        nc.sync.dma_start(cols_list[:], offs2)
        nc.sync.dma_start(out=wb_raw[:].bitcast(I32), in_=wb_words[0].bitcast(I32))
        nc.sync.dma_start(out=table[0][:], in_=table_rows[0])
        nc.sync.dma_start(table_list[:], offs3)
        load_scales(nc.sync, wb_scales_raw, wb_scales, range(4))
        nc.sync.dma_start(out=table[1][:], in_=table_rows[1])
        bias = sb.tile([P, I], F32, name="bias", align_bytes=64)
        nc.sync.dma_start(out=bias[:], in_=bi[0].partition_broadcast(P))

        floor = sb.tile([P, 1], F32, name="floor")
        nc.scalar.activation(out=floor[:], in_=one[:], func=ACT.Copy, scale=4.0 * I)

        xa_words = sb.tile([P, J], U32, name="xa_words", align_bytes=64)
        xa_scales = sb.tile([P, J], U8, name="xa_scales", align_bytes=64)
        xb_words = sb.tile([P, I], U32, name="xb_words", align_bytes=64)
        xb_scales = sb.tile([P, I], U8, name="xb_scales", align_bytes=64)
        wa_dealt = sb.tile([P, R], U32, name="wa_dealt", align_bytes=64)
        wa_scales_dealt = sb.tile([P, R], U8, name="wa_scales_dealt", align_bytes=64)
        wb_dealt = sb.tile([P, 2 * R], U8, name="wb_dealt", align_bytes=64)
        wb_scales_dealt = sb.tile([P, R], U8, name="wb_scales_dealt", align_bytes=64)

        def deal_scales(dealt, raw, slots):
            nc.vector.tensor_copy(
                out=dealt[:].rearrange("p (t n g) -> p n t g", t=PACK, g=16)[:, :, slots],
                in_=raw[:].rearrange("p (n g t) -> p n t g", t=PACK, g=16)[:, :, slots],
            )

        nc.vector.tensor_copy(xa_words[:], x_words[:].indirect(rows_list[:]))
        nc.vector.tensor_copy(xa_scales[:], x_scales[:].indirect(rows_list[:]))
        deal_scales(wa_scales_dealt, wa_scales_raw, slice(0, 2))
        deal_scales(wa_scales_dealt, wa_scales_raw, slice(2, 4))
        nc.vector.tensor_copy(xb_words[:], x_words[:].indirect(cols_list[:]))
        nc.vector.tensor_copy(xb_scales[:], x_scales[:].indirect(cols_list[:]))

        for u in range(2):
            nc.scalar.copy(
                out=wa_dealt[:].rearrange("p (t n g) -> p n t g", t=PACK, g=4)[:, :, 2 * u : 2 * u + 2],
                in_=wa_raw[:].rearrange("p (n g t) -> p n t g", t=PACK, g=4)[:, :, 2 * u : 2 * u + 2],
            )

        za = [ps.tile([P, PACK, P], F32, name=f"za{h}") for h in range(HALVES)]
        zb = [ps.tile([P, 2, I], F32, name=f"zb{u}") for u in range(2)]
        for h in range(HALVES):
            cols = slice(P * h, P * (h + 1))
            for t in range(PACK):
                slot = slice(P * t, P * (t + 1))
                nc.tensor.matmul_mx(
                    out=za[h][:, t, :],
                    lhsT=wa_dealt[:, slot].bitcast(E5M2),
                    lhsT_scale=wa_scales_dealt[:, slot],
                    rhs=xa_words[:, cols].bitcast(E4M3),
                    rhs_scale=xa_scales[:, cols],
                    start=True,
                    stop=True,
                )

        def pick(picked, u):
            for s in range(2):
                nc.scalar.activation(
                    out=picked[:, s, :],
                    in_=table[u][:, V * s : V * (s + 1)].indirect(table_list[:]),
                    func=ACT.Copy,
                )

        picked_low = sb.tile([P, 2, I], F32, name="picked_low", align_bytes=64)
        nc.scalar.copy(
            out=wb_dealt[:].bitcast(U16).rearrange("p (t n g) -> p n t g", t=PACK, g=8),
            in_=wb_raw[:].bitcast(U16).rearrange("p (n g t) -> p n t g", t=PACK, g=8),
        )
        pick(picked_low, 0)

        bundles = P // BUNDLE
        sums = [
            sb.tile([P, bundles, PACK], F32, name="sums0", align_bytes=64),
            reused.tile([P, bundles, PACK], F32, name="sums1", offset=0, align_bytes=64),
        ]
        means = [sb.tile([P, bundles, PACK], F32, name=f"means{h}") for h in range(HALVES)]
        diff_tile = sb.tile([P, HALVES * PACK * P], F32, name="diff", align_bytes=64)
        diff = diff_tile[:].rearrange("p (h t i) -> p h t i", h=HALVES, t=PACK)
        hb = [sb.tile([P, P * PACK], BF16, name=f"hb{h}", align_bytes=64) for h in range(HALVES)]
        ha_words = sb.tile([P, J], U32, name="ha_words", align_bytes=64)
        hb_words = sb.tile([P, I], U32, name="hb_words", align_bytes=64)
        hb_scales = sb.tile([P, I], U8, name="hb_scales", align_bytes=64)

        def bundle_means(h):
            nc.vector.tensor_reduce(
                out=sums[h][:],
                in_=za[h][:].rearrange("p t (e c) -> p e t c", c=BUNDLE),
                axis=AX.X,
                op=ALU.add,
            )
            nc.gpsimd.tensor_scalar(means[h][:], sums[h][:], 1.0 / BUNDLE, 0.0, ALU.mult, ALU.add)

        bundle_means(0)
        deal_scales(wb_scales_dealt, wb_scales_raw, slice(0, 4))
        bundle_means(1)
        ha_words32 = J * PACK // 2
        shared = reused.tile([P, ha_words32 - P + 2 * I], F32, name="shared", offset=R // 2, align_bytes=64)
        ha = shared[:, 0:ha_words32].bitcast(BF16)
        picked_high = shared[:, ha_words32 - P :].rearrange("p (s i) -> p s i", s=2)
        pick(picked_high, 1)
        for t in range(PACK):
            nc.tensor.matmul_mx(
                out=zb[t // 2][:, t % 2, :],
                lhsT=wb_dealt[:, 2 * P * t : 2 * P * (t + 1)].bitcast(E2M1),
                lhsT_scale=wb_scales_dealt[:, P * t : P * (t + 1)],
                rhs=xb_words[:].bitcast(E4M3),
                rhs_scale=xb_scales[:],
                start=True,
                stop=True,
            )

        def level(ha, h):
            nc.vector.tensor_tensor(
                out=ha.rearrange("p (e c t) -> p e c t", c=BUNDLE, t=PACK),
                in0=za[h][:].rearrange("p t (e c) -> p e c t", c=BUNDLE),
                in1=means[h][:].unsqueeze(2).to_broadcast([P, bundles, BUNDLE, PACK]),
                op=ALU.subtract,
            )

        def quantize(words, scales, values, h, fmt):
            cols = slice(P * h, P * (h + 1))
            nc.vector.quantize_mx(out=words[:, cols].bitcast(fmt), scales=scales[:, cols], in_=values)

        ha_scales = sb.tile([P, J], U8, name="ha_scales", align_bytes=64)
        level(ha[:, 0 : P * PACK], 0)
        nc.vector.tensor_tensor(
            out=diff[:, :, 0:2, :],
            in0=zb[0][:].rearrange("p t (h i) -> p h t i", h=HALVES),
            in1=picked_low[:].rearrange("p t (h i) -> p h t i", h=HALVES),
            op=ALU.subtract,
        )
        for h in range(HALVES):
            cols = slice(P * h, P * (h + 1))
            nc.vector.tensor_tensor(
                out=diff[:, h, 2:4, :], in0=zb[1][:, :, cols], in1=picked_high[:, :, cols], op=ALU.subtract
            )
            nc.scalar.activation(
                out=hb[h][:].rearrange("p (n g t) -> p n t g", g=4, t=PACK),
                in_=diff[:, h].rearrange("p t (n g) -> p n t g", g=4),
                func=ACT.Relu,
            )
        level(ha[:, P * PACK :], 1)
        quantize(hb_words, hb_scales, hb[0][:], 0, E5M2)
        nc.vector.quantize_mx(out=ha_words[:].bitcast(E4M3), scales=ha_scales[:], in_=ha)
        quantize(hb_words, hb_scales, hb[1][:], 1, E5M2)

        a0 = [ps.tile([P, I], F32, name=f"a0{h}") for h in range(HALVES)]
        a = [sb.tile([P, I], F32, name=f"a{h}", align_bytes=64) for h in range(HALVES)]
        dev = [sb.tile([P, I], F32, name=f"dev{h}", align_bytes=64) for h in range(HALVES)]
        size = [sb.tile([P, I], F32, name=f"size{h}", align_bytes=64) for h in range(HALVES)]
        y = [sb.tile([P, I], F32, name=f"y{h}", align_bytes=64) for h in range(HALVES)]
        total = [sb.tile([P, 1], F32, name=f"total{h}") for h in range(HALVES)]
        spread = [sb.tile([P, 1], F32, name=f"spread{h}") for h in range(HALVES)]
        divisor = [sb.tile([P, 1], F32, name=f"divisor{h}") for h in range(HALVES)]
        inverse = [sb.tile([P, 1], F32, name=f"inverse{h}") for h in range(HALVES)]
        for c in range(HALVES):
            cols = slice(P * c, P * (c + 1))
            for h in range(HALVES):
                rows = slice(P * h, P * (h + 1))
                nc.tensor.matmul_mx(
                    out=a0[h][:, cols],
                    lhsT=ha_words[:, rows].bitcast(E4M3),
                    lhsT_scale=ha_scales[:, rows],
                    rhs=hb_words[:, cols].bitcast(E5M2),
                    rhs_scale=hb_scales[:, cols],
                    start=True,
                    stop=True,
                )
        for h in range(HALVES):
            nc.vector.scalar_tensor_tensor(
                a[h][:], a0[h][:], 1.0, bias[:], ALU.mult, ALU.add, accum_out=total[h][:]
            )
            nc.scalar.activation(
                out=size[h][:],
                in_=a[h][:],
                func=ACT.Abs,
                scale=-float(I),
                bias=total[h][:],
                accum_out=spread[h][:],
            )
        for h in range(HALVES):
            nc.vector.tensor_scalar(dev[h][:], a[h][:], float(I), total[h][:], ALU.mult, ALU.subtract)
        for h in range(HALVES):
            nc.vector.tensor_scalar(divisor[h][:], spread[h][:], 1.0 / I, floor[:], ALU.mult, ALU.add)
            nc.vector.reciprocal(inverse[h][:], divisor[h][:])
        for h in range(HALVES):
            nc.vector.tensor_scalar(y[h][:], dev[h][:], inverse[h][:], None, ALU.mult)
            nc.sync.dma_start(out=out[P * h : P * (h + 1), :], in_=y[h][:])
